import numpy as np
import ml_dtypes


def mxq(x, axis, fmt="e4m3"):
    dtype, down = {"e4m3": (ml_dtypes.float8_e4m3fn, 7), "e5m2": (ml_dtypes.float8_e5m2, 14)}[fmt]
    v = np.moveaxis(np.asarray(x, np.float32).astype(ml_dtypes.bfloat16).astype(np.float64), axis, -1)
    blocks = v.reshape(v.shape[:-1] + (-1, 32))
    amax = np.abs(blocks).max(-1, keepdims=True)
    byte = np.maximum(np.where(amax > 0, np.frexp(amax)[1] - 1 + 127, 0) - down, 1)
    scale = np.exp2(byte - 127.0)
    codes = (blocks / scale).astype(np.float32).astype(dtype).astype(np.float64)
    return np.moveaxis((codes * scale).reshape(v.shape), -1, axis)


WIDE = False


def mx_kscale(k):
    if not WIDE:
        return np.ones(k)
    levels = np.array([10, -10, 5, -5, 0])
    if k % 512:
        return np.exp2(np.random.permutation(np.resize(levels, k // 32))).repeat(32)
    a = np.empty((k // 512, 16))
    for p in range(k // 512):
        a[p, :8] = np.random.permutation(np.resize(levels, 8))
        for g in range(8):
            far = levels[np.abs(levels - a[p, g]) >= 10]
            a[p, g + 8] = far[np.random.randint(len(far))]
    return np.exp2(a.ravel()).repeat(32)


def f64(x):
    return np.asarray(x).astype(np.float64)


def striped(idx):
    return np.tile(np.asarray(idx).reshape(-1, 16).T, (8, 1)).astype(np.uint16)


def unstriped(offs):
    return offs[:16].T.reshape(-1).astype(np.int64)


E2M1 = np.array([0.0, 0.5, 1.0, 1.5, 2.0, 3.0, 4.0, 6.0, -0.0, -0.5, -1.0, -1.5, -2.0, -3.0, -4.0, -6.0])


def pack_weight(w, fmt):
    k, n = w.shape
    w = f64(np.asarray(w, np.float32).astype(ml_dtypes.bfloat16)).reshape(k // 32, 32, n)
    amax = np.abs(w).max(1)
    if fmt == "e4m3":
        byte = np.frexp(amax)[1] - 1 + 127 - 7
    else:
        mant, ex = np.frexp(amax / 6.0)
        byte = np.where(mant > 0.5, ex, ex - 1) + 127
    byte = np.clip(np.where(amax > 0, byte, 1), 1, 254)
    scaled = (w * np.exp2(127.0 - byte)[:, None, :]).reshape(k, n).astype(np.float32)
    by_word = np.ascontiguousarray(scaled.reshape(k // 512, 128, 4, n).transpose(0, 1, 3, 2))
    if fmt == "e4m3":
        words = by_word.astype(ml_dtypes.float8_e4m3fn).view(np.uint8)
    else:
        c = by_word.astype(ml_dtypes.float4_e2m1fn).view(np.uint8) & 0xF
        words = (c[..., 0::2] | (c[..., 1::2] << 4)).reshape(k // 512, 128, 2 * n)
    return np.ascontiguousarray(words), np.ascontiguousarray(byte.astype(np.uint8).reshape(k // 512, 16, n))


def unpack_weight(words, scales, fmt):
    g, _, n = scales.shape
    words = np.ascontiguousarray(words).reshape(g, 128, n, -1)
    if fmt == "e4m3":
        vals = words.view(ml_dtypes.float8_e4m3fn).astype(np.float64)
    else:
        nib = np.empty((g, 128, n, 4), np.uint8)
        nib[..., 0::2] = words & 0xF
        nib[..., 1::2] = words >> 4
        vals = E2M1[nib]
    vals = vals * np.repeat(np.exp2(scales.astype(np.float64) - 127.0), 8, axis=1)[..., None]
    return vals.transpose(0, 1, 3, 2).reshape(g * 512, n)


def sigmoid(v):
    return 1.0 / (1.0 + np.exp(-v))


D, T, I, Q, E, Z, M = 512, 1024, 512, 512, 512, 1024, 1024


def setup_inputs():
    n = np.random.standard_normal
    idx = np.random.permutation(T)[:I]
    idx2 = np.random.permutation(Z)[:I]
    idx3 = np.random.permutation(M)[:I]
    fd = mx_kscale(D)
    fq = mx_kscale(Q)
    keysp = pack_weight(n((D, T)) / fd[:, None], "e4m3")
    return {
        "query": (n((D, Q)) * 1.0 / np.sqrt(D) * fd[:, None]).astype(np.float32),
        "query2": (n((D, Q)) * 1.0 / np.sqrt(D) * fd[:, None]).astype(np.float32),
        "keys_words": keysp[0],
        "keys_scales": keysp[1],
        "pages": (n((D, Z)) / fd[:, None]).astype(np.float32),
        "qs": (np.random.uniform(0.5, 2.0, (Q, 1)) * fq[:, None]).astype(np.float32),
        "msgs": (n((Q, E)) * 1 / np.sqrt(Q) / fq[:, None]).astype(np.float32),
        "old": (n((E, M)) * 1.0).astype(np.float32),
        "fade": (np.random.uniform(0.3, 0.9, (1, M))).astype(np.float32),
        "offs": striped(idx),
        "offs2": striped(idx2),
        "offs3": striped(idx3),
    }


def reference(query, query2, keys_words, keys_scales, pages, qs, msgs, old, fade, offs, offs2, offs3):
    idx = unstriped(offs)
    idx2 = unstriped(offs2)
    idx3 = unstriped(offs3)
    keysu = unpack_weight(keys_words, keys_scales, "e4m3")
    queryq = mxq(f64(query), 0, "e4m3")
    a = queryq.T @ keysu
    query2q = mxq(f64(query2), 0, "e4m3")
    pagesq = mxq(f64(pages), 0, "e4m3")
    h0 = query2q.T @ pagesq
    s = np.maximum(a[:, idx], h0[:, idx2])
    w = sigmoid(s)
    wq = w * f64(qs)
    msgsq = mxq(f64(msgs), 0, "e4m3")
    wqq = mxq(wq, 0, "e4m3")
    dl = msgsq.T @ wqq
    df = np.zeros((E, M))
    df[:, idx3] = dl
    y = f64(old) * f64(fade) + df
    return y

@@ -1,0 +1,281 @@
+from contextlib import ExitStack
+
+import concourse.mybir as mybir
+from concourse.masks import make_identity
+
+D, T, I, Q, E, Z, M = 512, 1024, 512, 512, 512, 1024, 1024
+FLOPS = 2 * D * Q * T + 2 * D * Q * Z + 2 * Q * E * I
+
+F32 = mybir.dt.float32
+BF16 = mybir.dt.bfloat16
+I32 = mybir.dt.int32
+U32 = mybir.dt.uint32
+U16 = mybir.dt.uint16
+U8 = mybir.dt.uint8
+FP8X4 = mybir.dt.float8_e4m3fn_x4
+MULT = mybir.AluOpType.mult
+ADD = mybir.AluOpType.add
+MAX = mybir.AluOpType.max
+SIGMOID = mybir.ActivationFunctionType.Sigmoid
+COPY = mybir.ActivationFunctionType.Copy
+
+P = 128
+PACK = 4
+BANK = 512
+HALF = I // 2
+HALF_COLS = HALF // 16
+HELD = {3: 2}
+GROUPS = [256,256]
+
+
+def tile_attend_crosslarger_delivered_lean_kernel(
+    tc, query, query2, keys_words, keys_scales, pages, qs, msgs, old, fade, offs, offs2, offs3, out
+):
+    nc = tc.nc
+    with ExitStack() as ctx:
+        keep = ctx.enter_context(tc.tile_pool(name="keep", bufs=1))
+        banks = ctx.enter_context(tc.psum_pool(name="banks", bufs=6))
+        fade_banks = ctx.enter_context(tc.psum_pool(name="fade_banks", bufs=1))
+
+        def sb(name, shape, dtype):
+            return keep.tile(shape, dtype, name=name, align_bytes=64)
+
+        def load_rows(name, src, c0, c1):
+            raw = sb(name, [P, PACK, c1 - c0], F32)
+            nc.sync.dma_start(out=raw[:], in_=src[:, c0:c1].rearrange("(p t) c -> p t c", t=PACK))
+            return raw
+
+        def copy(engine, dst, src):
+            if engine == "v":
+                nc.vector.tensor_copy(out=dst, in_=src)
+            elif engine == "g":
+                nc.gpsimd.tensor_scalar(out=dst, in0=src, scalar1=1.0, scalar2=0.0, op0=MULT, op1=ADD)
+            else:
+                nc.scalar.copy(out=dst, in_=src)
+
+        def round_dealt(engine, grouped, raw, s0, s1):
+            copy(
+                engine,
+                grouped[:, :, s0:s1, :].rearrange("p r s t -> p s t r"),
+                raw[:, :, s0 * PACK : s1 * PACK].rearrange("p t (s r) -> p s t r", r=PACK),
+            )
+
+        def round_plain(engine, grouped, raw):
+            copy(
+                engine,
+                grouped.rearrange("p (c i) t -> p c t i", i=PACK),
+                raw.rearrange("p t (c i) -> p c t i", i=PACK),
+            )
+
+        def quantise(name, flat):
+            width = flat.shape[1] // PACK
+            codes = sb(name + "_codes", [P, width], U32)
+            scales = sb(name + "_scales", [P, width], U8)
+            nc.vector.quantize_mx(out=codes[:].bitcast(FP8X4), scales=scales[:], in_=flat)
+            return codes, scales
+
+        def product(dst, stat, s0, mov, m0, n):
+            nc.tensor.matmul_mx(
+                out=dst,
+                lhsT=stat[0][:, s0 : s0 + P].bitcast(FP8X4),
+                lhsT_scale=stat[1][:, s0 : s0 + P],
+                rhs=mov[0][:, m0 : m0 + n].bitcast(FP8X4),
+                rhs_scale=mov[1][:, m0 : m0 + n],
+                start=True,
+                stop=True,
+            )
+
+        def load_list(name, src):
+            tile = sb(name, [P, I // 16], U16)
+            nc.sync.dma_start(tile[:], src)
+            return tile
+
+        key_scales = sb("key_scales", [P, T], U8)
+        q_raw = [load_rows(f"q_raw{h}", query, h * Q // 2, (h + 1) * Q // 2) for h in range(2)]
+        for quad in range(4):
+            nc.sync.dma_start(
+                out=key_scales[32 * quad : 32 * quad + 4, :].bitcast(I32),
+                in_=keys_scales[0, 4 * quad : 4 * quad + 4, :].bitcast(I32),
+            )
+        key_words = keys_words[0].rearrange("p c t -> p (c t)").bitcast(I32)
+        key_codes = sb("key_codes", [P, T], U32)
+        nc.sync.dma_start(out=key_codes[:, :BANK].bitcast(I32), in_=key_words[:, :BANK])
+        q2_raw = load_rows("q2_raw", query2, 0, Q)
+        nc.sync.dma_start(out=key_codes[:, BANK:].bitcast(I32), in_=key_words[:, BANK:])
+        token_list = load_list("token_list", offs)
+        pg_raw = [load_rows(f"pg_raw{n}", pages, n * BANK, (n + 1) * BANK) for n in range(2)]
+        page_list = load_list("page_list", offs2)
+        fade_cols = sb("fade_cols", [P, 2, PACK], F32)
+        nc.sync.dma_start(out=fade_cols[:], in_=fade.rearrange("o (h s c) -> s (o h) c", h=2, c=PACK))
+        msg_raw = load_rows("msg_raw", msgs, 0, E)
+        row_factor = sb("row_factor", [P, PACK], F32)
+        nc.sync.dma_start(out=row_factor[:], in_=qs.rearrange("(p r) o -> p (r o)", r=PACK))
+        column_list = load_list("column_list", offs3)
+        result = []
+        for e in range(E // P):
+            tile = sb(f"result{e}", [P, M], F32)
+            nc.sync.dma_start(out=tile[:], in_=old[e * P : (e + 1) * P, :])
+            result.append(tile)
+
+        placed = []
+        for e in range(E // P):
+            tile = sb(f"placed{e}", [P, M], F32)
+            nc.vector.memset(tile[:], 0.0)
+            placed.append(tile)
+        identity = sb("identity", [P, P], F32)
+        make_identity(nc, identity[:])
+
+        q_bf = sb("q_bf", [P, PACK, P, PACK], BF16)
+        for h in range(2):
+            round_dealt("vv"[h], q_bf[:, :, h * P // 2 : (h + 1) * P // 2, :], q_raw[h][:], 0, P // 2)
+        q_mx = [quantise(f"q{r}", q_bf[:, r].rearrange("p s t -> p (s t)")) for r in range(PACK)]
+        a_sb = [sb(f"a{r}", [P, T], F32) for r in range(PACK)]
+        weight = sb("weight", [P, PACK, I], F32)
+        for n in range(2):
+            for r in range(PACK):
+                bank = banks.tile([P, BANK], F32, name="bank")
+                product(bank[:], q_mx[r], 0, (key_codes, key_scales), n * BANK, BANK)
+                copy("ssvsvsss"[4 * n + r], a_sb[r][:, n * BANK : (n + 1) * BANK], bank[:])
+        for r in range(PACK):
+            nc.scalar.activation(out=weight[:, r, :], in_=a_sb[r][:].indirect(token_list[:]), func=SIGMOID)
+
+        q2_bf = sb("q2_bf", [P, PACK, P, PACK], BF16)
+        round_dealt("v", q2_bf, q2_raw, 0, P)
+        q2_mx = quantise("q2", q2_bf[:].rearrange("p r s t -> p (r s t)"))
+        h_sb = [sb(f"h{r}", [P, Z], F32) for r in range(PACK)]
+        pg_mx = []
+        for n in range(2):
+            pg_bf = sb(f"pg_bf{n}", [P, BANK, PACK], BF16)
+            for k in range(1):
+                w = BANK // 1
+                round_plain("vv"[n], pg_bf[:, k * w : (k + 1) * w, :], pg_raw[n][:, :, k * w : (k + 1) * w])
+            pg_mx.append(quantise(f"pg{n}", pg_bf[:].rearrange("p c t -> p (c t)")))
+        for n in range(2):
+            for r in range(PACK):
+                bank = banks.tile([P, BANK], F32, name="bank")
+                product(bank[:], q2_mx, r * P, pg_mx[n], 0, BANK)
+                copy("svssssvs"[4 * n + r], h_sb[r][:, n * BANK : (n + 1) * BANK], bank[:])
+
+        fade_bank = []
+        for h in range(2):
+            bank = fade_banks.tile([P, PACK, P], F32, name=f"fade_bank{h}")
+            for c in range(PACK):
+                nc.tensor.transpose(bank[:, c, :], fade_cols[:, h, c : c + 1].to_broadcast([P, P]), identity[:])
+            fade_bank.append(bank)
+
+        msg_bf = sb("msg_bf", [P, E, PACK], BF16)
+        for k in range(1):
+            w = E // 1
+            round_plain("v", msg_bf[:, k * w : (k + 1) * w, :], msg_raw[:, :, k * w : (k + 1) * w])
+        msg_mx = quantise("msg", msg_bf[:].rearrange("p c t -> p (c t)"))
+
+        page_weight = sb("page_weight", [P, PACK, I], F32)
+        sums = {}
+
+        tops, wqs, dl_banks, faded = {}, {}, {}, {}
+
+        def span(group):
+            return slice(sum(GROUPS[:group]), sum(GROUPS[: group + 1]))
+
+        def look_up(group):
+            slots = span(group)
+            for r in range(PACK):
+                nc.scalar.activation(
+                    out=page_weight[:, r, slots],
+                    in_=h_sb[r][:].indirect(page_list[:, slots.start // 16 : slots.stop // 16]),
+                    func=SIGMOID,
+                )
+
+        def larger(group):
+            slots = span(group)
+            tops[group] = keep.tile([P, PACK, GROUPS[group]], F32, name=f"top{group}", tag="top", align_bytes=64)
+            for r0 in range(0, PACK, 2):
+                rows = slice(r0, r0 + 2)
+                nc.vector.tensor_tensor(
+                    out=tops[group][:, rows, :], in0=weight[:, rows, slots], in1=page_weight[:, rows, slots], op=MAX
+                )
+
+        def weigh(group):
+            n = GROUPS[group]
+            wq_bf = keep.tile([P, n, PACK], BF16, name=f"wq_bf{group}", tag=f"link{group + 1}", align_bytes=64)
+            nc.vector.tensor_tensor(
+                out=wq_bf[:].rearrange("p (c i) r -> p c r i", i=PACK),
+                in0=tops[group][:].rearrange("p r (c i) -> p c r i", i=PACK),
+                in1=row_factor[:].unsqueeze(1).unsqueeze(3).to_broadcast([P, n // PACK, PACK, PACK]),
+                op=MULT,
+            )
+            wqs[group] = wq_bf
+
+        def deliver(group):
+            n = GROUPS[group]
+            wq_mx = quantise(f"wq{group}", wqs[group][:].rearrange("p c r -> p (c r)"))
+            per_bank = BANK // n
+            for e0 in range(0, E // P, per_bank):
+                bank = banks.tile([P, BANK], F32, name="bank")
+                for j in range(per_bank):
+                    product(bank[:, j * n : (j + 1) * n], msg_mx, (e0 + j) * P, wq_mx, 0, n)
+                dl_banks[group, e0 // per_bank] = bank
+
+        def stage(engine, group, k):
+            n = GROUPS[group]
+            per_bank = BANK // n
+            staged = sb(f"sums{group}{k}", [P, BANK], F32)
+            copy(engine, staged[:], dl_banks[group, k][:])
+            for j in range(per_bank):
+                sums[k * per_bank + j, group] = staged[:, j * n : (j + 1) * n]
+
+        def scatter(engine, e, group):
+            first, n = sum(GROUPS[:group]), GROUPS[group]
+            window = placed[e][:].indirect(column_list[:, first // 16 : (first + n) // 16])
+            if engine == "v":
+                nc.vector.tensor_copy(out=window, in_=sums[e, group])
+            else:
+                nc.scalar.activation(out=window, in_=sums[e, group], func=COPY)
+
+        def fade_old(e, halves=(0, 1)):
+            for h in halves:
+                if e in HELD and e not in faded:
+                    faded[e] = keep.tile([P, M], F32, name=f"faded{e}", tag=f"link{HELD[e]}", align_bytes=64)
+                dst = faded.get(e, result[e])
+                nc.vector.tensor_tensor(
+                    out=dst[:, h * BANK : (h + 1) * BANK].rearrange("p (s c) -> p s c", c=PACK),
+                    in0=result[e][:, h * BANK : (h + 1) * BANK].rearrange("p (s c) -> p s c", c=PACK),
+                    in1=fade_bank[h][:].rearrange("p c s -> p s c"),
+                    op=MULT,
+                )
+
+        def finish(engine, e, halves=(0, 1)):
+            adder = nc.vector if engine == "v" else nc.gpsimd
+            for h in halves:
+                cols = slice(h * BANK, (h + 1) * BANK)
+                adder.tensor_tensor(out=result[e][:, cols], in0=faded.get(e, result[e])[:, cols], in1=placed[e][:, cols], op=ADD)
+                nc.sync.dma_start(out=out[e * P : (e + 1) * P, cols], in_=result[e][:, cols])
+
+        fade_old(0)
+        fade_old(1)
+        fade_old(2)
+        look_up(0)
+        look_up(1)
+        larger(0)
+        weigh(0)
+        deliver(0)
+        stage("s", 0, 0)
+        stage("s", 0, 1)
+        larger(1)
+        weigh(1)
+        deliver(1)
+        fade_old(3)
+        scatter("s", 0, 0)
+        scatter("s", 1, 0)
+        scatter("s", 2, 0)
+        stage("v", 1, 0)
+        stage("v", 1, 1)
+        scatter("v", 0, 1)
+        scatter("v", 1, 1)
+        scatter("s", 2, 1)
+        scatter("s", 3, 0)
+        scatter("s", 3, 1)
+        finish("v", 0)
+        finish("v", 1)
+        finish("v", 2)
+        finish("v", 3)

@@ -124,6 +124,8 @@ def tile_attend_crosslarger_delivered_lean_kernel(
             placed.append(tile)
         identity = sb("identity", [P, P], F32)
         make_identity(nc, identity[:])
+        warm = sb("warm", [P, 1], F32)
+        nc.scalar.activation(out=warm[:], in_=identity[:, 0:1], func=SIGMOID)
 
         q_bf = sb("q_bf", [P, PACK, P, PACK], BF16)
         for h in range(2):

@@ -22,10 +22,9 @@ COPY = mybir.ActivationFunctionType.Copy
 P = 128
 PACK = 4
 BANK = 512
-HALF = I // 2
-HALF_COLS = HALF // 16
-HELD = {3: 2}
-GROUPS = [256,256]
+LIST_ROWS = 16
+E_TILES = E // P
+GROUPS = (256, 256)
 
 
 def tile_attend_crosslarger_delivered_lean_kernel(
@@ -34,37 +33,38 @@ def tile_attend_crosslarger_delivered_lean_kernel(
     nc = tc.nc
     with ExitStack() as ctx:
         keep = ctx.enter_context(tc.tile_pool(name="keep", bufs=1))
-        banks = ctx.enter_context(tc.psum_pool(name="banks", bufs=6))
-        fade_banks = ctx.enter_context(tc.psum_pool(name="fade_banks", bufs=1))
+        banks = ctx.enter_context(tc.psum_pool(name="banks", bufs=8))
 
-        def sb(name, shape, dtype):
-            return keep.tile(shape, dtype, name=name, align_bytes=64)
+        def sb(name, shape, dtype, tag=None):
+            return keep.tile(shape, dtype, name=name, tag=tag or name, align_bytes=64)
 
-        def load_rows(name, src, c0, c1):
-            raw = sb(name, [P, PACK, c1 - c0], F32)
-            nc.sync.dma_start(out=raw[:], in_=src[:, c0:c1].rearrange("(p t) c -> p t c", t=PACK))
+        def halves(width):
+            return (slice(0, width // 2), slice(width // 2, width))
+
+        def load_rows(name, src, cols):
+            raw = sb(name, [P, PACK, cols.stop - cols.start], F32)
+            nc.sync.dma_start(out=raw[:], in_=src[:, cols].rearrange("(p t) c -> p t c", t=PACK))
             return raw
 
-        def copy(engine, dst, src):
-            if engine == "v":
-                nc.vector.tensor_copy(out=dst, in_=src)
-            elif engine == "g":
-                nc.gpsimd.tensor_scalar(out=dst, in0=src, scalar1=1.0, scalar2=0.0, op0=MULT, op1=ADD)
-            else:
-                nc.scalar.copy(out=dst, in_=src)
+        def load_list(name, src):
+            tile = sb(name, [P, I // LIST_ROWS], U16)
+            nc.sync.dma_start(tile[:], src)
+            return tile
 
-        def round_dealt(engine, grouped, raw, s0, s1):
-            copy(
-                engine,
-                grouped[:, :, s0:s1, :].rearrange("p r s t -> p s t r"),
-                raw[:, :, s0 * PACK : s1 * PACK].rearrange("p t (s r) -> p s t r", r=PACK),
+        def load_old(e):
+            tile = sb(f"old{e}", [P, M], F32)
+            nc.sync.dma_start(out=tile[:], in_=old[e * P : (e + 1) * P, :])
+            return tile
+
+        def round_dealt(grouped, raw):
+            nc.vector.tensor_copy(
+                out=grouped.rearrange("p r s t -> p s t r"), in_=raw.rearrange("p t (s r) -> p s t r", r=PACK)
             )
 
-        def round_plain(engine, grouped, raw):
-            copy(
-                engine,
-                grouped.rearrange("p (c i) t -> p c t i", i=PACK),
-                raw.rearrange("p t (c i) -> p c t i", i=PACK),
+        def round_plain(grouped, raw):
+            nc.vector.tensor_copy(
+                out=grouped.rearrange("p (c i) t -> p c t i", i=PACK),
+                in_=raw.rearrange("p t (c i) -> p c t i", i=PACK),
             )
 
         def quantise(name, flat):
@@ -74,24 +74,27 @@ def tile_attend_crosslarger_delivered_lean_kernel(
             nc.vector.quantize_mx(out=codes[:].bitcast(FP8X4), scales=scales[:], in_=flat)
             return codes, scales
 
-        def product(dst, stat, s0, mov, m0, n):
+        def product(dst, stationary, first, moving, cols):
             nc.tensor.matmul_mx(
                 out=dst,
-                lhsT=stat[0][:, s0 : s0 + P].bitcast(FP8X4),
-                lhsT_scale=stat[1][:, s0 : s0 + P],
-                rhs=mov[0][:, m0 : m0 + n].bitcast(FP8X4),
-                rhs_scale=mov[1][:, m0 : m0 + n],
+                lhsT=stationary[0][:, first : first + P].bitcast(FP8X4),
+                lhsT_scale=stationary[1][:, first : first + P],
+                rhs=moving[0][:, cols].bitcast(FP8X4),
+                rhs_scale=moving[1][:, cols],
                 start=True,
                 stop=True,
             )
 
-        def load_list(name, src):
-            tile = sb(name, [P, I // 16], U16)
-            nc.sync.dma_start(tile[:], src)
-            return tile
+        def empty(on_vector, dst, bank):
+            if on_vector:
+                nc.vector.tensor_copy(out=dst, in_=bank)
+            else:
+                nc.scalar.copy(out=dst, in_=bank)
 
+        fade_cols = sb("fade_cols", [P, 2, PACK], F32)
+        nc.scalar.dma_start(out=fade_cols[:], in_=fade.rearrange("o (h s c) -> s (o h) c", h=2, c=PACK))
+        q_raw = [load_rows(f"q_raw{h}", query, cols) for h, cols in enumerate(halves(Q))]
         key_scales = sb("key_scales", [P, T], U8)
-        q_raw = [load_rows(f"q_raw{h}", query, h * Q // 2, (h + 1) * Q // 2) for h in range(2)]
         for quad in range(4):
             nc.sync.dma_start(
                 out=key_scales[32 * quad : 32 * quad + 4, :].bitcast(I32),
@@ -99,185 +102,150 @@ def tile_attend_crosslarger_delivered_lean_kernel(
             )
         key_words = keys_words[0].rearrange("p c t -> p (c t)").bitcast(I32)
         key_codes = sb("key_codes", [P, T], U32)
-        nc.sync.dma_start(out=key_codes[:, :BANK].bitcast(I32), in_=key_words[:, :BANK])
-        q2_raw = load_rows("q2_raw", query2, 0, Q)
-        nc.sync.dma_start(out=key_codes[:, BANK:].bitcast(I32), in_=key_words[:, BANK:])
+        for cols in halves(T):
+            nc.sync.dma_start(out=key_codes[:, cols].bitcast(I32), in_=key_words[:, cols])
+        old_sb = [load_old(0)]
         token_list = load_list("token_list", offs)
-        pg_raw = [load_rows(f"pg_raw{n}", pages, n * BANK, (n + 1) * BANK) for n in range(2)]
+        q2_raw = load_rows("q2_raw", query2, slice(0, Q))
+        pg_raw = [load_rows(f"pg_raw{n}", pages, cols) for n, cols in enumerate(halves(Z))]
         page_list = load_list("page_list", offs2)
-        fade_cols = sb("fade_cols", [P, 2, PACK], F32)
-        nc.sync.dma_start(out=fade_cols[:], in_=fade.rearrange("o (h s c) -> s (o h) c", h=2, c=PACK))
-        msg_raw = load_rows("msg_raw", msgs, 0, E)
+        old_sb.append(load_old(1))
+        msg_raw = load_rows("msg_raw", msgs, slice(0, E))
         row_factor = sb("row_factor", [P, PACK], F32)
         nc.sync.dma_start(out=row_factor[:], in_=qs.rearrange("(p r) o -> p (r o)", r=PACK))
         column_list = load_list("column_list", offs3)
-        result = []
-        for e in range(E // P):
-            tile = sb(f"result{e}", [P, M], F32)
-            nc.sync.dma_start(out=tile[:], in_=old[e * P : (e + 1) * P, :])
-            result.append(tile)
+        old_sb.extend(load_old(e) for e in range(2, E_TILES))
 
-        placed = []
-        for e in range(E // P):
-            tile = sb(f"placed{e}", [P, M], F32)
+        placed = [sb(f"placed{e}", [P, M], F32) for e in range(E_TILES)]
+        for tile in placed:
             nc.vector.memset(tile[:], 0.0)
-            placed.append(tile)
         identity = sb("identity", [P, P], F32)
         make_identity(nc, identity[:])
         warm = sb("warm", [P, 1], F32)
         nc.scalar.activation(out=warm[:], in_=identity[:, 0:1], func=SIGMOID)
 
+        fade_row = sb("fade_row", [P, M], F32)
+        for h, cols in enumerate(halves(M)):
+            bank = banks.tile([P, PACK, P], F32, name="bank")
+            for c in range(PACK):
+                nc.tensor.transpose(bank[:, c, :], fade_cols[:, h, c : c + 1].to_broadcast([P, P]), identity[:])
+            nc.scalar.copy(
+                out=fade_row[:, cols].rearrange("p (s c) -> p s c", c=PACK), in_=bank[:].rearrange("p c s -> p s c")
+            )
+
+        def fade_old(engine, dst, e):
+            for cols in halves(M):
+                engine.tensor_tensor(out=dst[:, cols], in0=old_sb[e][:, cols], in1=fade_row[:, cols], op=MULT)
+
         q_bf = sb("q_bf", [P, PACK, P, PACK], BF16)
-        for h in range(2):
-            round_dealt("vv"[h], q_bf[:, :, h * P // 2 : (h + 1) * P // 2, :], q_raw[h][:], 0, P // 2)
-        q_mx = [quantise(f"q{r}", q_bf[:, r].rearrange("p s t -> p (s t)")) for r in range(PACK)]
+        for h, part in enumerate(halves(P)):
+            round_dealt(q_bf[:, :, part, :], q_raw[h][:])
+        q_mx = [quantise(f"q_tile{r}", q_bf[:, r].rearrange("p s t -> p (s t)")) for r in range(PACK)]
         a_sb = [sb(f"a{r}", [P, T], F32) for r in range(PACK)]
-        weight = sb("weight", [P, PACK, I], F32)
-        for n in range(2):
-            for r in range(PACK):
-                bank = banks.tile([P, BANK], F32, name="bank")
-                product(bank[:], q_mx[r], 0, (key_codes, key_scales), n * BANK, BANK)
-                copy("ssvsvsss"[4 * n + r], a_sb[r][:, n * BANK : (n + 1) * BANK], bank[:])
+        token_weight = sb("token_weight", [P, PACK, I], F32)
         for r in range(PACK):
-            nc.scalar.activation(out=weight[:, r, :], in_=a_sb[r][:].indirect(token_list[:]), func=SIGMOID)
+            for n, cols in enumerate(halves(T)):
+                bank = banks.tile([P, BANK], F32, name="bank")
+                product(bank[:], q_mx[r], 0, (key_codes, key_scales), cols)
+                empty("svsvsvss"[2 * r + n] == "v", a_sb[r][:, cols], bank[:])
+        for r in range(PACK):
+            nc.scalar.activation(out=token_weight[:, r, :], in_=a_sb[r][:].indirect(token_list[:]), func=SIGMOID)
+        faded = {0: old_sb[0]}
+        fade_old(nc.vector, faded[0], 0)
 
         q2_bf = sb("q2_bf", [P, PACK, P, PACK], BF16)
-        round_dealt("v", q2_bf, q2_raw, 0, P)
+        round_dealt(q2_bf[:], q2_raw[:])
         q2_mx = quantise("q2", q2_bf[:].rearrange("p r s t -> p (r s t)"))
         h_sb = [sb(f"h{r}", [P, Z], F32) for r in range(PACK)]
         pg_mx = []
         for n in range(2):
             pg_bf = sb(f"pg_bf{n}", [P, BANK, PACK], BF16)
-            for k in range(1):
-                w = BANK // 1
-                round_plain("vv"[n], pg_bf[:, k * w : (k + 1) * w, :], pg_raw[n][:, :, k * w : (k + 1) * w])
+            round_plain(pg_bf[:], pg_raw[n][:])
             pg_mx.append(quantise(f"pg{n}", pg_bf[:].rearrange("p c t -> p (c t)")))
-        for n in range(2):
+        for n, cols in enumerate(halves(Z)):
             for r in range(PACK):
                 bank = banks.tile([P, BANK], F32, name="bank")
-                product(bank[:], q2_mx, r * P, pg_mx[n], 0, BANK)
-                copy("svssssvs"[4 * n + r], h_sb[r][:, n * BANK : (n + 1) * BANK], bank[:])
-
-        fade_bank = []
-        for h in range(2):
-            bank = fade_banks.tile([P, PACK, P], F32, name=f"fade_bank{h}")
-            for c in range(PACK):
-                nc.tensor.transpose(bank[:, c, :], fade_cols[:, h, c : c + 1].to_broadcast([P, P]), identity[:])
-            fade_bank.append(bank)
+                product(bank[:], q2_mx, r * P, pg_mx[n], slice(0, BANK))
+                empty("ssvvvvss"[4 * n + r] == "v", h_sb[r][:, cols], bank[:])
+        faded[1] = sb("faded1", [P, M], F32, tag="pg_bf1")
+        fade_old(nc.gpsimd, faded[1], 1)
 
         msg_bf = sb("msg_bf", [P, E, PACK], BF16)
-        for k in range(1):
-            w = E // 1
-            round_plain("v", msg_bf[:, k * w : (k + 1) * w, :], msg_raw[:, :, k * w : (k + 1) * w])
+        round_plain(msg_bf[:], msg_raw[:])
         msg_mx = quantise("msg", msg_bf[:].rearrange("p c t -> p (c t)"))
 
-        page_weight = sb("page_weight", [P, PACK, I], F32)
-        sums = {}
+        spans = [slice(sum(GROUPS[:g]), sum(GROUPS[: g + 1])) for g in range(len(GROUPS))]
 
-        tops, wqs, dl_banks, faded = {}, {}, {}, {}
+        def entries(slots):
+            return slice(slots.start // LIST_ROWS, slots.stop // LIST_ROWS)
 
-        def span(group):
-            return slice(sum(GROUPS[:group]), sum(GROUPS[: group + 1]))
-
-        def look_up(group):
-            slots = span(group)
+        page_weight = []
+        for g, slots in enumerate(spans):
+            page_weight.append(sb(f"page_weight{g}", [P, PACK, GROUPS[g]], F32))
             for r in range(PACK):
                 nc.scalar.activation(
-                    out=page_weight[:, r, slots],
-                    in_=h_sb[r][:].indirect(page_list[:, slots.start // 16 : slots.stop // 16]),
-                    func=SIGMOID,
+                    out=page_weight[g][:, r, :], in_=h_sb[r][:].indirect(page_list[:, entries(slots)]), func=SIGMOID
                 )
-
-        def larger(group):
-            slots = span(group)
-            tops[group] = keep.tile([P, PACK, GROUPS[group]], F32, name=f"top{group}", tag="top", align_bytes=64)
-            for r0 in range(0, PACK, 2):
-                rows = slice(r0, r0 + 2)
+        dl_banks = []
+        for g, slots in enumerate(spans):
+            n = GROUPS[g]
+            weight = sb(f"weight{g}", [P, PACK, n], F32, tag="weight")
+            step = BANK // n
+            for r in range(0, PACK, step):
+                rows = slice(r, r + step)
                 nc.vector.tensor_tensor(
-                    out=tops[group][:, rows, :], in0=weight[:, rows, slots], in1=page_weight[:, rows, slots], op=MAX
+                    out=weight[:, rows, :], in0=token_weight[:, rows, slots], in1=page_weight[g][:, rows, :], op=MAX
                 )
-
-        def weigh(group):
-            n = GROUPS[group]
-            wq_bf = keep.tile([P, n, PACK], BF16, name=f"wq_bf{group}", tag=f"link{group + 1}", align_bytes=64)
+            wq_bf = sb(f"wq_bf{g}", [P, n, PACK], BF16)
             nc.vector.tensor_tensor(
                 out=wq_bf[:].rearrange("p (c i) r -> p c r i", i=PACK),
-                in0=tops[group][:].rearrange("p r (c i) -> p c r i", i=PACK),
+                in0=weight[:].rearrange("p r (c i) -> p c r i", i=PACK),
                 in1=row_factor[:].unsqueeze(1).unsqueeze(3).to_broadcast([P, n // PACK, PACK, PACK]),
                 op=MULT,
             )
-            wqs[group] = wq_bf
+            wq_mx = quantise(f"wq{g}", wq_bf[:].rearrange("p c r -> p (c r)"))
+            dl_banks.append([])
+            for first in range(0, E_TILES, step):
+                bank = banks.tile([P, step, n], F32, name="bank")
+                for j in range(step):
+                    product(bank[:, j, :], msg_mx, (first + j) * P, wq_mx, slice(0, n))
+                dl_banks[g].append(bank)
 
-        def deliver(group):
-            n = GROUPS[group]
-            wq_mx = quantise(f"wq{group}", wqs[group][:].rearrange("p c r -> p (c r)"))
-            per_bank = BANK // n
-            for e0 in range(0, E // P, per_bank):
-                bank = banks.tile([P, BANK], F32, name="bank")
-                for j in range(per_bank):
-                    product(bank[:, j * n : (j + 1) * n], msg_mx, (e0 + j) * P, wq_mx, 0, n)
-                dl_banks[group, e0 // per_bank] = bank
+        late = sb("faded_late", [P, 2, M], F32, tag=f"wq_bf{len(GROUPS) - 1}")
+        for e in (2, 3):
+            faded[e] = late[:, e - 2, :]
+            fade_old(nc.gpsimd, faded[e], e)
 
-        def stage(engine, group, k):
-            n = GROUPS[group]
-            per_bank = BANK // n
-            staged = sb(f"sums{group}{k}", [P, BANK], F32)
-            copy(engine, staged[:], dl_banks[group, k][:])
-            for j in range(per_bank):
-                sums[k * per_bank + j, group] = staged[:, j * n : (j + 1) * n]
+        dl = {}
 
-        def scatter(engine, e, group):
-            first, n = sum(GROUPS[:group]), GROUPS[group]
-            window = placed[e][:].indirect(column_list[:, first // 16 : (first + n) // 16])
-            if engine == "v":
-                nc.vector.tensor_copy(out=window, in_=sums[e, group])
+        def stage(on_vector, g, k):
+            step = BANK // GROUPS[g]
+            staged = sb(f"dl{g}_{k}", [P, step, GROUPS[g]], F32)
+            empty(on_vector, staged[:], dl_banks[g][k][:])
+            for j in range(step):
+                dl[k * step + j, g] = staged[:, j, :]
+
+        def scatter(on_vector, e, g):
+            window = placed[e][:].indirect(column_list[:, entries(spans[g])])
+            if on_vector:
+                nc.vector.tensor_copy(out=window, in_=dl[e, g])
             else:
-                nc.scalar.activation(out=window, in_=sums[e, group], func=COPY)
+                nc.scalar.activation(out=window, in_=dl[e, g], func=COPY)
 
-        def fade_old(e, halves=(0, 1)):
-            for h in halves:
-                if e in HELD and e not in faded:
-                    faded[e] = keep.tile([P, M], F32, name=f"faded{e}", tag=f"link{HELD[e]}", align_bytes=64)
-                dst = faded.get(e, result[e])
-                nc.vector.tensor_tensor(
-                    out=dst[:, h * BANK : (h + 1) * BANK].rearrange("p (s c) -> p s c", c=PACK),
-                    in0=result[e][:, h * BANK : (h + 1) * BANK].rearrange("p (s c) -> p s c", c=PACK),
-                    in1=fade_bank[h][:].rearrange("p c s -> p s c"),
-                    op=MULT,
-                )
+        stage(False, 0, 0)
+        scatter(False, 0, 0)
+        scatter(False, 1, 0)
+        stage(False, 0, 1)
+        scatter(False, 2, 0)
+        scatter(False, 3, 0)
+        stage(True, 1, 0)
+        stage(True, 1, 1)
+        scatter(True, 0, 1)
+        scatter(True, 1, 1)
+        scatter(False, 2, 1)
+        scatter(False, 3, 1)
 
-        def finish(engine, e, halves=(0, 1)):
-            adder = nc.vector if engine == "v" else nc.gpsimd
-            for h in halves:
-                cols = slice(h * BANK, (h + 1) * BANK)
-                adder.tensor_tensor(out=result[e][:, cols], in0=faded.get(e, result[e])[:, cols], in1=placed[e][:, cols], op=ADD)
-                nc.sync.dma_start(out=out[e * P : (e + 1) * P, cols], in_=result[e][:, cols])
-
-        fade_old(0)
-        fade_old(1)
-        fade_old(2)
-        look_up(0)
-        look_up(1)
-        larger(0)
-        weigh(0)
-        deliver(0)
-        stage("s", 0, 0)
-        stage("s", 0, 1)
-        larger(1)
-        weigh(1)
-        deliver(1)
-        fade_old(3)
-        scatter("s", 0, 0)
-        scatter("s", 1, 0)
-        scatter("s", 2, 0)
-        stage("v", 1, 0)
-        stage("v", 1, 1)
-        scatter("v", 0, 1)
-        scatter("v", 1, 1)
-        scatter("s", 2, 1)
-        scatter("s", 3, 0)
-        scatter("s", 3, 1)
-        finish("v", 0)
-        finish("v", 1)
-        finish("v", 2)
-        finish("v", 3)
+        for e in range(E_TILES):
+            for cols in halves(M):
+                nc.vector.tensor_tensor(out=old_sb[e][:, cols], in0=faded[e][:, cols], in1=placed[e][:, cols], op=ADD)
+                nc.sync.dma_start(out=out[e * P : (e + 1) * P, cols], in_=old_sb[e][:, cols])

@@ -22,9 +22,17 @@ COPY = mybir.ActivationFunctionType.Copy
 P = 128
 PACK = 4
 BANK = 512
+BLOCK = 32
+QUADRANT = 32
+SCALE_ROWS = 4
 LIST_ROWS = 16
 E_TILES = E // P
-GROUPS = (256, 256)
+GROUP = I // 2
+PAIR = BANK // GROUP
+FADE_BANKS = M // BANK
+ROTATING_BANKS = 8 - FADE_BANKS
+SCALAR_QUERY_SHARE = 40
+SCALAR_PAGE_BANKS = 3
 
 
 def tile_attend_crosslarger_delivered_lean_kernel(
@@ -33,45 +41,53 @@ def tile_attend_crosslarger_delivered_lean_kernel(
     nc = tc.nc
     with ExitStack() as ctx:
         keep = ctx.enter_context(tc.tile_pool(name="keep", bufs=1))
-        banks = ctx.enter_context(tc.psum_pool(name="banks", bufs=8))
+        banks = ctx.enter_context(tc.psum_pool(name="banks", bufs=ROTATING_BANKS))
+        fade_banks = ctx.enter_context(tc.psum_pool(name="fade_banks", bufs=1))
 
-        def sb(name, shape, dtype, tag=None):
+        def sbuf(name, shape, dtype, tag=None):
             return keep.tile(shape, dtype, name=name, tag=tag or name, align_bytes=64)
 
         def halves(width):
             return (slice(0, width // 2), slice(width // 2, width))
 
+        def entries(slots):
+            return slice(slots.start // LIST_ROWS, slots.stop // LIST_ROWS)
+
         def load_rows(name, src, cols):
-            raw = sb(name, [P, PACK, cols.stop - cols.start], F32)
+            raw = sbuf(name, [P, PACK, cols.stop - cols.start], F32)
             nc.sync.dma_start(out=raw[:], in_=src[:, cols].rearrange("(p t) c -> p t c", t=PACK))
             return raw
 
         def load_list(name, src):
-            tile = sb(name, [P, I // LIST_ROWS], U16)
+            tile = sbuf(name, [P, I // LIST_ROWS], U16)
             nc.sync.dma_start(tile[:], src)
             return tile
 
         def load_old(e):
-            tile = sb(f"old{e}", [P, M], F32)
+            tile = sbuf(f"old{e}", [P, M], F32)
             nc.sync.dma_start(out=tile[:], in_=old[e * P : (e + 1) * P, :])
             return tile
 
-        def round_dealt(grouped, raw):
-            nc.vector.tensor_copy(
-                out=grouped.rearrange("p r s t -> p s t r"), in_=raw.rearrange("p t (s r) -> p s t r", r=PACK)
-            )
+        def round_dealt(copy, grouped, raw):
+            copy(out=grouped.rearrange("p r s t -> p s t r"), in_=raw.rearrange("p t (s r) -> p s t r", r=PACK))
 
-        def round_plain(grouped, raw):
-            nc.vector.tensor_copy(
+        def round_plain(copy, grouped, raw):
+            copy(
                 out=grouped.rearrange("p (c i) t -> p c t i", i=PACK),
                 in_=raw.rearrange("p t (c i) -> p c t i", i=PACK),
             )
 
-        def quantise(name, flat):
+        def quantise(name, flat, pieces=1, tag=None):
             width = flat.shape[1] // PACK
-            codes = sb(name + "_codes", [P, width], U32)
-            scales = sb(name + "_scales", [P, width], U8)
-            nc.vector.quantize_mx(out=codes[:].bitcast(FP8X4), scales=scales[:], in_=flat)
+            codes = sbuf(name + "_codes", [P, width], U32, tag=tag)
+            scales = sbuf(name + "_scales", [P, width], U8)
+            step = width // pieces
+            for c in range(0, width, step):
+                nc.vector.quantize_mx(
+                    out=codes[:, c : c + step].bitcast(FP8X4),
+                    scales=scales[:, c : c + step],
+                    in_=flat[:, PACK * c : PACK * (c + step)],
+                )
             return codes, scales
 
         def product(dst, stationary, first, moving, cols):
@@ -86,164 +102,185 @@ def tile_attend_crosslarger_delivered_lean_kernel(
             )
 
         def empty(on_vector, dst, bank):
-            if on_vector:
-                nc.vector.tensor_copy(out=dst, in_=bank)
-            else:
-                nc.scalar.copy(out=dst, in_=bank)
+            copy = nc.vector.tensor_copy if on_vector else nc.scalar.copy
+            copy(out=dst, in_=bank)
 
-        fade_cols = sb("fade_cols", [P, 2, PACK], F32)
-        nc.scalar.dma_start(out=fade_cols[:], in_=fade.rearrange("o (h s c) -> s (o h) c", h=2, c=PACK))
-        q_raw = [load_rows(f"q_raw{h}", query, cols) for h, cols in enumerate(halves(Q))]
-        key_scales = sb("key_scales", [P, T], U8)
-        for quad in range(4):
+        fade_cols = sbuf("fade_cols", [P, FADE_BANKS, PACK], F32)
+        nc.sync.dma_start(out=fade_cols[:], in_=fade.rearrange("o (h s c) -> s (o h) c", h=FADE_BANKS, c=PACK))
+        q_raw = load_rows("q_raw", query, slice(0, Q))
+        key_scales = sbuf("key_scales", [P, T], U8)
+        for row in range(SCALE_ROWS):
             nc.sync.dma_start(
-                out=key_scales[32 * quad : 32 * quad + 4, :].bitcast(I32),
-                in_=keys_scales[0, 4 * quad : 4 * quad + 4, :].bitcast(I32),
+                out=key_scales[row:P:QUADRANT, :].bitcast(I32),
+                in_=keys_scales[0, row : D // BLOCK : SCALE_ROWS, :].bitcast(I32),
             )
+        key_codes = sbuf("key_codes", [P, T], U32)
         key_words = keys_words[0].rearrange("p c t -> p (c t)").bitcast(I32)
-        key_codes = sb("key_codes", [P, T], U32)
         for cols in halves(T):
             nc.sync.dma_start(out=key_codes[:, cols].bitcast(I32), in_=key_words[:, cols])
-        old_sb = [load_old(0)]
-        token_list = load_list("token_list", offs)
         q2_raw = load_rows("q2_raw", query2, slice(0, Q))
+        token_list = load_list("token_list", offs)
         pg_raw = [load_rows(f"pg_raw{n}", pages, cols) for n, cols in enumerate(halves(Z))]
         page_list = load_list("page_list", offs2)
-        old_sb.append(load_old(1))
+        old_sb = [load_old(0)]
         msg_raw = load_rows("msg_raw", msgs, slice(0, E))
-        row_factor = sb("row_factor", [P, PACK], F32)
+        row_factor = sbuf("row_factor", [P, PACK], F32)
         nc.sync.dma_start(out=row_factor[:], in_=qs.rearrange("(p r) o -> p (r o)", r=PACK))
         column_list = load_list("column_list", offs3)
-        old_sb.extend(load_old(e) for e in range(2, E_TILES))
+        old_sb.extend(load_old(e) for e in range(1, E_TILES))
 
-        placed = [sb(f"placed{e}", [P, M], F32) for e in range(E_TILES)]
+        warm_in = sbuf("warm_in", [P, 1], F32)
+        nc.vector.memset(warm_in[:], 0.0)
+        warm_out = sbuf("warm_out", [P, 1], F32)
+        nc.scalar.activation(out=warm_out[:], in_=warm_in[:], func=SIGMOID)
+
+        placed = [sbuf(f"placed{e}", [P, M], F32) for e in range(E_TILES)]
         for tile in placed:
             nc.vector.memset(tile[:], 0.0)
-        identity = sb("identity", [P, P], F32)
+        identity = sbuf("identity", [P, P], F32)
         make_identity(nc, identity[:])
-        warm = sb("warm", [P, 1], F32)
-        nc.scalar.activation(out=warm[:], in_=identity[:, 0:1], func=SIGMOID)
 
-        fade_row = sb("fade_row", [P, M], F32)
+        fade_row = sbuf("fade_row", [P, M], F32)
+        fade_bank = []
         for h, cols in enumerate(halves(M)):
-            bank = banks.tile([P, PACK, P], F32, name="bank")
+            bank = fade_banks.tile([P, PACK, P], F32, name=f"fade_bank{h}")
             for c in range(PACK):
                 nc.tensor.transpose(bank[:, c, :], fade_cols[:, h, c : c + 1].to_broadcast([P, P]), identity[:])
-            nc.scalar.copy(
-                out=fade_row[:, cols].rearrange("p (s c) -> p s c", c=PACK), in_=bank[:].rearrange("p c s -> p s c")
-            )
+            fade_bank.append(bank[:].rearrange("p c s -> p s c"))
+            nc.scalar.copy(out=fade_row[:, cols].rearrange("p (s c) -> p s c", c=PACK), in_=fade_bank[h])
 
-        def fade_old(engine, dst, e):
+        def fade_on_gpsimd(dst, e):
             for cols in halves(M):
-                engine.tensor_tensor(out=dst[:, cols], in0=old_sb[e][:, cols], in1=fade_row[:, cols], op=MULT)
+                nc.gpsimd.tensor_tensor(out=dst[:, cols], in0=old_sb[e][:, cols], in1=fade_row[:, cols], op=MULT)
 
-        q_bf = sb("q_bf", [P, PACK, P, PACK], BF16)
-        for h, part in enumerate(halves(P)):
-            round_dealt(q_bf[:, :, part, :], q_raw[h][:])
-        q_mx = [quantise(f"q_tile{r}", q_bf[:, r].rearrange("p s t -> p (s t)")) for r in range(PACK)]
-        a_sb = [sb(f"a{r}", [P, T], F32) for r in range(PACK)]
-        token_weight = sb("token_weight", [P, PACK, I], F32)
+        def fade_on_vector(dst, e):
+            for h, cols in enumerate(halves(M)):
+                nc.vector.tensor_tensor(
+                    out=dst[:, cols].rearrange("p (s c) -> p s c", c=PACK),
+                    in0=old_sb[e][:, cols].rearrange("p (s c) -> p s c", c=PACK),
+                    in1=fade_bank[h],
+                    op=MULT,
+                )
+
+        q_bf = sbuf("q_bf", [P, PACK, P, PACK], BF16)
+        cut = SCALAR_QUERY_SHARE
+        round_dealt(nc.vector.tensor_copy, q_bf[:, :, cut:, :], q_raw[:, :, cut * PACK :])
+        round_dealt(nc.scalar.copy, q_bf[:, :, :cut, :], q_raw[:, :, : cut * PACK])
+        q_mx = [
+            quantise(f"q_tile{r}", q_bf[:, r].rearrange("p s t -> p (s t)"), tag=None if r else "fade_cols")
+            for r in range(PACK)
+        ]
+        a_sb = [sbuf(f"a{r}", [P, T], F32) for r in range(PACK)]
+        token_weight = sbuf("token_weight", [P, PACK, I], F32)
         for r in range(PACK):
             for n, cols in enumerate(halves(T)):
                 bank = banks.tile([P, BANK], F32, name="bank")
                 product(bank[:], q_mx[r], 0, (key_codes, key_scales), cols)
-                empty("svsvsvss"[2 * r + n] == "v", a_sb[r][:, cols], bank[:])
+                empty(n == 1 and r < PACK - 1, a_sb[r][:, cols], bank[:])
         for r in range(PACK):
             nc.scalar.activation(out=token_weight[:, r, :], in_=a_sb[r][:].indirect(token_list[:]), func=SIGMOID)
-        faded = {0: old_sb[0]}
-        fade_old(nc.vector, faded[0], 0)
 
-        q2_bf = sb("q2_bf", [P, PACK, P, PACK], BF16)
-        round_dealt(q2_bf[:], q2_raw[:])
+        q2_bf = sbuf("q2_bf", [P, PACK, P, PACK], BF16)
+        round_dealt(nc.vector.tensor_copy, q2_bf[:], q2_raw[:])
         q2_mx = quantise("q2", q2_bf[:].rearrange("p r s t -> p (r s t)"))
-        h_sb = [sb(f"h{r}", [P, Z], F32) for r in range(PACK)]
+        h_sb = [sbuf(f"h{r}", [P, Z], F32) for r in range(PACK)]
         pg_mx = []
-        for n in range(2):
-            pg_bf = sb(f"pg_bf{n}", [P, BANK, PACK], BF16)
-            round_plain(pg_bf[:], pg_raw[n][:])
-            pg_mx.append(quantise(f"pg{n}", pg_bf[:].rearrange("p c t -> p (c t)")))
+        for n in range(len(pg_raw)):
+            pg_bf = sbuf(f"pg_bf{n}", [P, BANK, PACK], BF16)
+            for cols in halves(BANK):
+                round_plain(nc.vector.tensor_copy, pg_bf[:, cols, :], pg_raw[n][:, :, cols])
+            pg_mx.append(quantise(f"pg{n}", pg_bf[:].rearrange("p c t -> p (c t)"), pieces=2))
         for n, cols in enumerate(halves(Z)):
             for r in range(PACK):
                 bank = banks.tile([P, BANK], F32, name="bank")
                 product(bank[:], q2_mx, r * P, pg_mx[n], slice(0, BANK))
-                empty("ssvvvvss"[4 * n + r] == "v", h_sb[r][:, cols], bank[:])
-        faded[1] = sb("faded1", [P, M], F32, tag="pg_bf1")
-        fade_old(nc.gpsimd, faded[1], 1)
+                empty(PACK * n + r >= SCALAR_PAGE_BANKS, h_sb[r][:, cols], bank[:])
 
-        msg_bf = sb("msg_bf", [P, E, PACK], BF16)
-        round_plain(msg_bf[:], msg_raw[:])
-        msg_mx = quantise("msg", msg_bf[:].rearrange("p c t -> p (c t)"))
+        faded = [sbuf("faded_first", [P, M], F32, tag=f"pg_bf{len(pg_raw) - 1}")]
+        fade_on_gpsimd(faded[0], 0)
 
-        spans = [slice(sum(GROUPS[:g]), sum(GROUPS[: g + 1])) for g in range(len(GROUPS))]
+        def round_messages(k, copy, tag=None):
+            rounded = sbuf(f"msg_bf{k}", [P, E // 2, PACK], BF16, tag=tag)
+            round_plain(copy, rounded[:], msg_raw[:, :, halves(E)[k]])
+            return rounded[:].rearrange("p c t -> p (c t)")
 
-        def entries(slots):
-            return slice(slots.start // LIST_ROWS, slots.stop // LIST_ROWS)
+        groups = halves(I)
+        row_pairs = halves(PACK)
 
-        page_weight = []
-        for g, slots in enumerate(spans):
-            page_weight.append(sb(f"page_weight{g}", [P, PACK, GROUPS[g]], F32))
+        def gather_pages(g):
+            tiles = [
+                sbuf(f"page_weight{g}_{k}", [P, PACK // 2, GROUP], F32, tag=f"page_weight{k}")
+                for k in range(len(row_pairs))
+            ]
             for r in range(PACK):
                 nc.scalar.activation(
-                    out=page_weight[g][:, r, :], in_=h_sb[r][:].indirect(page_list[:, entries(slots)]), func=SIGMOID
+                    out=tiles[r // 2][:, r % 2, :],
+                    in_=h_sb[r][:].indirect(page_list[:, entries(groups[g])]),
+                    func=SIGMOID,
                 )
-        dl_banks = []
-        for g, slots in enumerate(spans):
-            n = GROUPS[g]
-            weight = sb(f"weight{g}", [P, PACK, n], F32, tag="weight")
-            step = BANK // n
-            for r in range(0, PACK, step):
-                rows = slice(r, r + step)
-                nc.vector.tensor_tensor(
-                    out=weight[:, rows, :], in0=token_weight[:, rows, slots], in1=page_weight[g][:, rows, :], op=MAX
-                )
-            wq_bf = sb(f"wq_bf{g}", [P, n, PACK], BF16)
+            return tiles
+
+        def larger(g, k, weight, page_weight):
+            rows = row_pairs[k]
+            nc.vector.tensor_tensor(
+                out=weight[:, rows, :], in0=token_weight[:, rows, groups[g]], in1=page_weight[k][:], op=MAX
+            )
+
+        def times_row_factor(g, weight):
+            wq_bf = sbuf(f"wq_bf{g}", [P, GROUP, PACK], BF16)
             nc.vector.tensor_tensor(
                 out=wq_bf[:].rearrange("p (c i) r -> p c r i", i=PACK),
                 in0=weight[:].rearrange("p r (c i) -> p c r i", i=PACK),
-                in1=row_factor[:].unsqueeze(1).unsqueeze(3).to_broadcast([P, n // PACK, PACK, PACK]),
+                in1=row_factor[:].unsqueeze(1).unsqueeze(3).to_broadcast([P, GROUP // PACK, PACK, PACK]),
                 op=MULT,
             )
-            wq_mx = quantise(f"wq{g}", wq_bf[:].rearrange("p c r -> p (c r)"))
+            return wq_bf[:].rearrange("p c r -> p (c r)")
+
+        page_weight = gather_pages(0)
+        weight = sbuf("weight0", [P, PACK, GROUP], F32, tag="weight")
+        larger(0, 0, weight, page_weight)
+        msg_bf = round_messages(0, nc.vector.tensor_copy)
+        larger(0, 1, weight, page_weight)
+        msg_mx = [quantise("msg0", msg_bf)]
+        wq_mx = [quantise("wq0", times_row_factor(0, weight))]
+
+        page_weight = gather_pages(1)
+        weight = sbuf("weight1", [P, PACK, GROUP], F32, tag="weight")
+        for k in range(len(row_pairs)):
+            larger(1, k, weight, page_weight)
+        msg_bf = round_messages(1, nc.scalar.copy, tag=f"h{PACK - 1}")
+        wq_bf = times_row_factor(1, weight)
+        msg_mx.append(quantise("msg1", msg_bf))
+        wq_mx.append(quantise("wq1", wq_bf))
+
+        dl_banks = []
+        for group_mx in wq_mx:
             dl_banks.append([])
-            for first in range(0, E_TILES, step):
-                bank = banks.tile([P, step, n], F32, name="bank")
-                for j in range(step):
-                    product(bank[:, j, :], msg_mx, (first + j) * P, wq_mx, slice(0, n))
-                dl_banks[g].append(bank)
+            for half_mx in msg_mx:
+                bank = banks.tile([P, PAIR, GROUP], F32, name="bank")
+                for j in range(PAIR):
+                    product(bank[:, j, :], half_mx, j * P, group_mx, slice(0, GROUP))
+                dl_banks[-1].append(bank)
 
-        late = sb("faded_late", [P, 2, M], F32, tag=f"wq_bf{len(GROUPS) - 1}")
-        for e in (2, 3):
-            faded[e] = late[:, e - 2, :]
-            fade_old(nc.gpsimd, faded[e], e)
+        late = sbuf("faded_late", [P, E_TILES - 1, M], F32, tag=f"wq_bf{len(groups) - 1}")
+        faded.extend(late[:, e - 1, :] for e in range(1, E_TILES))
+        fade_on_vector(faded[1], 1)
+        for e in range(2, E_TILES):
+            fade_on_gpsimd(faded[e], e)
 
-        dl = {}
-
-        def stage(on_vector, g, k):
-            step = BANK // GROUPS[g]
-            staged = sb(f"dl{g}_{k}", [P, step, GROUPS[g]], F32)
-            empty(on_vector, staged[:], dl_banks[g][k][:])
-            for j in range(step):
-                dl[k * step + j, g] = staged[:, j, :]
-
-        def scatter(on_vector, e, g):
-            window = placed[e][:].indirect(column_list[:, entries(spans[g])])
-            if on_vector:
-                nc.vector.tensor_copy(out=window, in_=dl[e, g])
-            else:
-                nc.scalar.activation(out=window, in_=dl[e, g], func=COPY)
-
-        stage(False, 0, 0)
-        scatter(False, 0, 0)
-        scatter(False, 1, 0)
-        stage(False, 0, 1)
-        scatter(False, 2, 0)
-        scatter(False, 3, 0)
-        stage(True, 1, 0)
-        stage(True, 1, 1)
-        scatter(True, 0, 1)
-        scatter(True, 1, 1)
-        scatter(False, 2, 1)
-        scatter(False, 3, 1)
+        for g, slots in enumerate(groups):
+            last = g == len(groups) - 1
+            dl = []
+            for k, bank in enumerate(dl_banks[g]):
+                staged = sbuf(f"dl{g}_{k}", [P, PAIR, GROUP], F32)
+                empty(last, staged[:], bank[:])
+                dl.extend(staged[:, j, :] for j in range(PAIR))
+            for e in range(E_TILES):
+                window = placed[e][:].indirect(column_list[:, entries(slots)])
+                if last and e < E_TILES // 2:
+                    nc.vector.tensor_copy(out=window, in_=dl[e])
+                else:
+                    nc.scalar.activation(out=window, in_=dl[e], func=COPY)
 
         for e in range(E_TILES):
             for cols in halves(M):

@@ -77,17 +77,17 @@ def tile_attend_crosslarger_delivered_lean_kernel(
                 in_=raw.rearrange("p t (c i) -> p c t i", i=PACK),
             )
 
-        def quantise(name, flat, pieces=1, tag=None):
-            width = flat.shape[1] // PACK
+        def quantise(name, pieces, tag=None):
+            width = sum(piece.shape[1] for piece in pieces)
             codes = sbuf(name + "_codes", [P, width], U32, tag=tag)
             scales = sbuf(name + "_scales", [P, width], U8)
-            step = width // pieces
-            for c in range(0, width, step):
+            first = 0
+            for piece in pieces:
+                cols = slice(first, first + piece.shape[1])
                 nc.vector.quantize_mx(
-                    out=codes[:, c : c + step].bitcast(FP8X4),
-                    scales=scales[:, c : c + step],
-                    in_=flat[:, PACK * c : PACK * (c + step)],
+                    out=codes[:, cols].bitcast(FP8X4), scales=scales[:, cols], in_=piece.rearrange("p c t -> p (c t)")
                 )
+                first = cols.stop
             return codes, scales
 
         def product(dst, stationary, first, moving, cols):
@@ -120,7 +120,9 @@ def tile_attend_crosslarger_delivered_lean_kernel(
             nc.sync.dma_start(out=key_codes[:, cols].bitcast(I32), in_=key_words[:, cols])
         q2_raw = load_rows("q2_raw", query2, slice(0, Q))
         token_list = load_list("token_list", offs)
-        pg_raw = [load_rows(f"pg_raw{n}", pages, cols) for n, cols in enumerate(halves(Z))]
+        page_loads = (slice(0, Z // 2), slice(Z // 2, 3 * Z // 4), slice(3 * Z // 4, Z))
+        pg_tiles = [load_rows(f"pg_raw{n}", pages, cols) for n, cols in enumerate(page_loads)]
+        pg_raw = [[pg_tiles[0][:, :, cols] for cols in halves(BANK)], [tile[:] for tile in pg_tiles[1:]]]
         page_list = load_list("page_list", offs2)
         old_sb = [load_old(0)]
         msg_raw = load_rows("msg_raw", msgs, slice(0, E))
@@ -167,7 +169,7 @@ def tile_attend_crosslarger_delivered_lean_kernel(
         round_dealt(nc.vector.tensor_copy, q_bf[:, :, cut:, :], q_raw[:, :, cut * PACK :])
         round_dealt(nc.scalar.copy, q_bf[:, :, :cut, :], q_raw[:, :, : cut * PACK])
         q_mx = [
-            quantise(f"q_tile{r}", q_bf[:, r].rearrange("p s t -> p (s t)"), tag=None if r else "fade_cols")
+            quantise(f"q_tile{r}", [q_bf[:, r]], tag=None if r else "fade_cols")
             for r in range(PACK)
         ]
         a_sb = [sbuf(f"a{r}", [P, T], F32) for r in range(PACK)]
@@ -182,27 +184,29 @@ def tile_attend_crosslarger_delivered_lean_kernel(
 
         q2_bf = sbuf("q2_bf", [P, PACK, P, PACK], BF16)
         round_dealt(nc.vector.tensor_copy, q2_bf[:], q2_raw[:])
-        q2_mx = quantise("q2", q2_bf[:].rearrange("p r s t -> p (r s t)"))
-        h_sb = [sbuf(f"h{r}", [P, Z], F32) for r in range(PACK)]
+        q2_mx = quantise("q2", [q2_bf[:].rearrange("p r s t -> p (r s) t")])
         pg_mx = []
-        for n in range(len(pg_raw)):
-            pg_bf = sbuf(f"pg_bf{n}", [P, BANK, PACK], BF16)
-            for cols in halves(BANK):
-                round_plain(nc.vector.tensor_copy, pg_bf[:, cols, :], pg_raw[n][:, :, cols])
-            pg_mx.append(quantise(f"pg{n}", pg_bf[:].rearrange("p c t -> p (c t)"), pieces=2))
+        for n, quarters in enumerate(pg_raw):
+            pg_bf = [sbuf(f"pg_bf{n}_{k}", [P, BANK // 2, PACK], BF16) for k in range(len(quarters))]
+            for rounded, raw in zip(pg_bf, quarters):
+                round_plain(nc.vector.tensor_copy, rounded[:], raw)
+            tag = f"pg_raw{len(page_loads) - 1}" if n else None
+            pg_mx.append(quantise(f"pg{n}", [rounded[:] for rounded in pg_bf], tag=tag))
+        last_h_tag = "pg_bf1_0"
+        h_sb = [sbuf(f"h{r}", [P, Z], F32, tag=last_h_tag if r == PACK - 1 else None) for r in range(PACK)]
         for n, cols in enumerate(halves(Z)):
             for r in range(PACK):
                 bank = banks.tile([P, BANK], F32, name="bank")
                 product(bank[:], q2_mx, r * P, pg_mx[n], slice(0, BANK))
                 empty(PACK * n + r >= SCALAR_PAGE_BANKS, h_sb[r][:, cols], bank[:])
 
-        faded = [sbuf("faded_first", [P, M], F32, tag=f"pg_bf{len(pg_raw) - 1}")]
+        faded = [sbuf("faded_first", [P, M], F32, tag="pg_bf1_1")]
         fade_on_gpsimd(faded[0], 0)
 
         def round_messages(k, copy, tag=None):
             rounded = sbuf(f"msg_bf{k}", [P, E // 2, PACK], BF16, tag=tag)
             round_plain(copy, rounded[:], msg_raw[:, :, halves(E)[k]])
-            return rounded[:].rearrange("p c t -> p (c t)")
+            return [rounded[:]]
 
         groups = halves(I)
         row_pairs = halves(PACK)
@@ -228,13 +232,14 @@ def tile_attend_crosslarger_delivered_lean_kernel(
 
         def times_row_factor(g, weight):
             wq_bf = sbuf(f"wq_bf{g}", [P, GROUP, PACK], BF16)
-            nc.vector.tensor_tensor(
-                out=wq_bf[:].rearrange("p (c i) r -> p c r i", i=PACK),
-                in0=weight[:].rearrange("p r (c i) -> p c r i", i=PACK),
-                in1=row_factor[:].unsqueeze(1).unsqueeze(3).to_broadcast([P, GROUP // PACK, PACK, PACK]),
-                op=MULT,
-            )
-            return wq_bf[:].rearrange("p c r -> p (c r)")
+            for cols in halves(GROUP):
+                nc.vector.tensor_tensor(
+                    out=wq_bf[:, cols, :].rearrange("p (c i) r -> p c r i", i=PACK),
+                    in0=weight[:, :, cols].rearrange("p r (c i) -> p c r i", i=PACK),
+                    in1=row_factor[:].unsqueeze(1).unsqueeze(3).to_broadcast([P, GROUP // 2 // PACK, PACK, PACK]),
+                    op=MULT,
+                )
+            return [wq_bf[:, cols, :] for cols in halves(GROUP)]
 
         page_weight = gather_pages(0)
         weight = sbuf("weight0", [P, PACK, GROUP], F32, tag="weight")
@@ -248,7 +253,7 @@ def tile_attend_crosslarger_delivered_lean_kernel(
         weight = sbuf("weight1", [P, PACK, GROUP], F32, tag="weight")
         for k in range(len(row_pairs)):
             larger(1, k, weight, page_weight)
-        msg_bf = round_messages(1, nc.scalar.copy, tag=f"h{PACK - 1}")
+        msg_bf = round_messages(1, nc.scalar.copy, tag=last_h_tag)
         wq_bf = times_row_factor(1, weight)
         msg_mx.append(quantise("msg1", msg_bf))
         wq_mx.append(quantise("wq1", wq_bf))

from contextlib import ExitStack

import concourse.mybir as mybir
from concourse.masks import make_identity

D, T, I, Q, E, Z, M = 512, 1024, 512, 512, 512, 1024, 1024
FLOPS = 2 * D * Q * T + 2 * D * Q * Z + 2 * Q * E * I

F32 = mybir.dt.float32
BF16 = mybir.dt.bfloat16
I32 = mybir.dt.int32
U32 = mybir.dt.uint32
U16 = mybir.dt.uint16
U8 = mybir.dt.uint8
FP8X4 = mybir.dt.float8_e4m3fn_x4
MULT = mybir.AluOpType.mult
ADD = mybir.AluOpType.add
MAX = mybir.AluOpType.max
SIGMOID = mybir.ActivationFunctionType.Sigmoid
COPY = mybir.ActivationFunctionType.Copy

P = 128
PACK = 4
BANK = 512
BLOCK = 32
QUADRANT = 32
SCALE_ROWS = 4
LIST_ROWS = 16
E_TILES = E // P
GROUP = I // 2
PAIR = BANK // GROUP
FADE_BANKS = M // BANK
ROTATING_BANKS = 8 - FADE_BANKS
SCALAR_QUERY_SHARE = 40
SCALAR_PAGE_BANKS = 3


def tile_attend_crosslarger_delivered_lean_kernel(
    tc, query, query2, keys_words, keys_scales, pages, qs, msgs, old, fade, offs, offs2, offs3, out
):
    nc = tc.nc
    with ExitStack() as ctx:
        keep = ctx.enter_context(tc.tile_pool(name="keep", bufs=1))
        banks = ctx.enter_context(tc.psum_pool(name="banks", bufs=ROTATING_BANKS))
        fade_banks = ctx.enter_context(tc.psum_pool(name="fade_banks", bufs=1))

        def sbuf(name, shape, dtype, tag=None):
            return keep.tile(shape, dtype, name=name, tag=tag or name, align_bytes=64)

        def halves(width):
            return (slice(0, width // 2), slice(width // 2, width))

        def entries(slots):
            return slice(slots.start // LIST_ROWS, slots.stop // LIST_ROWS)

        def load_rows(name, src, cols):
            raw = sbuf(name, [P, PACK, cols.stop - cols.start], F32)
            nc.sync.dma_start(out=raw[:], in_=src[:, cols].rearrange("(p t) c -> p t c", t=PACK))
            return raw

        def load_list(name, src):
            tile = sbuf(name, [P, I // LIST_ROWS], U16)
            nc.sync.dma_start(tile[:], src)
            return tile

        def load_old(e):
            tile = sbuf(f"old{e}", [P, M], F32)
            nc.sync.dma_start(out=tile[:], in_=old[e * P : (e + 1) * P, :])
            return tile

        def round_dealt(copy, grouped, raw):
            copy(out=grouped.rearrange("p r s t -> p s t r"), in_=raw.rearrange("p t (s r) -> p s t r", r=PACK))

        def round_plain(copy, grouped, raw):
            copy(
                out=grouped.rearrange("p (c i) t -> p c t i", i=PACK),
                in_=raw.rearrange("p t (c i) -> p c t i", i=PACK),
            )

        def quantise(name, pieces, tag=None):
            width = sum(piece.shape[1] for piece in pieces)
            codes = sbuf(name + "_codes", [P, width], U32, tag=tag)
            scales = sbuf(name + "_scales", [P, width], U8)
            first = 0
            for piece in pieces:
                cols = slice(first, first + piece.shape[1])
                nc.vector.quantize_mx(
                    out=codes[:, cols].bitcast(FP8X4), scales=scales[:, cols], in_=piece.rearrange("p c t -> p (c t)")
                )
                first = cols.stop
            return codes, scales

        def product(dst, stationary, first, moving, cols):
            nc.tensor.matmul_mx(
                out=dst,
                lhsT=stationary[0][:, first : first + P].bitcast(FP8X4),
                lhsT_scale=stationary[1][:, first : first + P],
                rhs=moving[0][:, cols].bitcast(FP8X4),
                rhs_scale=moving[1][:, cols],
                start=True,
                stop=True,
            )

        def empty(on_vector, dst, bank):
            copy = nc.vector.tensor_copy if on_vector else nc.scalar.copy
            copy(out=dst, in_=bank)

        fade_cols = sbuf("fade_cols", [P, FADE_BANKS, PACK], F32)
        nc.sync.dma_start(out=fade_cols[:], in_=fade.rearrange("o (h s c) -> s (o h) c", h=FADE_BANKS, c=PACK))
        q_raw = load_rows("q_raw", query, slice(0, Q))
        key_scales = sbuf("key_scales", [P, T], U8)
        for row in range(SCALE_ROWS):
            nc.sync.dma_start(
                out=key_scales[row:P:QUADRANT, :].bitcast(I32),
                in_=keys_scales[0, row : D // BLOCK : SCALE_ROWS, :].bitcast(I32),
            )
        key_codes = sbuf("key_codes", [P, T], U32)
        key_words = keys_words[0].rearrange("p c t -> p (c t)").bitcast(I32)
        for cols in halves(T):
            nc.sync.dma_start(out=key_codes[:, cols].bitcast(I32), in_=key_words[:, cols])
        q2_raw = load_rows("q2_raw", query2, slice(0, Q))
        token_list = load_list("token_list", offs)
        page_loads = (slice(0, Z // 2), slice(Z // 2, 3 * Z // 4), slice(3 * Z // 4, Z))
        pg_tiles = [load_rows(f"pg_raw{n}", pages, cols) for n, cols in enumerate(page_loads)]
        pg_raw = [[pg_tiles[0][:, :, cols] for cols in halves(BANK)], [tile[:] for tile in pg_tiles[1:]]]
        page_list = load_list("page_list", offs2)
        old_sb = [load_old(0)]
        msg_raw = load_rows("msg_raw", msgs, slice(0, E))
        row_factor = sbuf("row_factor", [P, PACK], F32)
        nc.sync.dma_start(out=row_factor[:], in_=qs.rearrange("(p r) o -> p (r o)", r=PACK))
        column_list = load_list("column_list", offs3)
        old_sb.extend(load_old(e) for e in range(1, E_TILES))

        warm_in = sbuf("warm_in", [P, 1], F32)
        nc.vector.memset(warm_in[:], 0.0)
        warm_out = sbuf("warm_out", [P, 1], F32)
        nc.scalar.activation(out=warm_out[:], in_=warm_in[:], func=SIGMOID)

        placed = [sbuf(f"placed{e}", [P, M], F32) for e in range(E_TILES)]
        for tile in placed:
            nc.vector.memset(tile[:], 0.0)
        identity = sbuf("identity", [P, P], F32)
        make_identity(nc, identity[:])

        fade_row = sbuf("fade_row", [P, M], F32)
        fade_bank = []
        for h, cols in enumerate(halves(M)):
            bank = fade_banks.tile([P, PACK, P], F32, name=f"fade_bank{h}")
            for c in range(PACK):
                nc.tensor.transpose(bank[:, c, :], fade_cols[:, h, c : c + 1].to_broadcast([P, P]), identity[:])
            fade_bank.append(bank[:].rearrange("p c s -> p s c"))
            nc.scalar.copy(out=fade_row[:, cols].rearrange("p (s c) -> p s c", c=PACK), in_=fade_bank[h])

        def fade_on_gpsimd(dst, e):
            for cols in halves(M):
                nc.gpsimd.tensor_tensor(out=dst[:, cols], in0=old_sb[e][:, cols], in1=fade_row[:, cols], op=MULT)

        def fade_on_vector(dst, e):
            for h, cols in enumerate(halves(M)):
                nc.vector.tensor_tensor(
                    out=dst[:, cols].rearrange("p (s c) -> p s c", c=PACK),
                    in0=old_sb[e][:, cols].rearrange("p (s c) -> p s c", c=PACK),
                    in1=fade_bank[h],
                    op=MULT,
                )

        q_bf = sbuf("q_bf", [P, PACK, P, PACK], BF16)
        cut = SCALAR_QUERY_SHARE
        round_dealt(nc.vector.tensor_copy, q_bf[:, :, cut:, :], q_raw[:, :, cut * PACK :])
        round_dealt(nc.scalar.copy, q_bf[:, :, :cut, :], q_raw[:, :, : cut * PACK])
        q_mx = [
            quantise(f"q_tile{r}", [q_bf[:, r]], tag=None if r else "fade_cols")
            for r in range(PACK)
        ]
        a_sb = [sbuf(f"a{r}", [P, T], F32) for r in range(PACK)]
        token_weight = sbuf("token_weight", [P, PACK, I], F32)
        for r in range(PACK):
            for n, cols in enumerate(halves(T)):
                bank = banks.tile([P, BANK], F32, name="bank")
                product(bank[:], q_mx[r], 0, (key_codes, key_scales), cols)
                empty(n == 1 and r < PACK - 1, a_sb[r][:, cols], bank[:])
        for r in range(PACK):
            nc.scalar.activation(out=token_weight[:, r, :], in_=a_sb[r][:].indirect(token_list[:]), func=SIGMOID)

        q2_bf = sbuf("q2_bf", [P, PACK, P, PACK], BF16)
        round_dealt(nc.vector.tensor_copy, q2_bf[:], q2_raw[:])
        q2_mx = quantise("q2", [q2_bf[:].rearrange("p r s t -> p (r s) t")])
        pg_mx = []
        for n, quarters in enumerate(pg_raw):
            pg_bf = [sbuf(f"pg_bf{n}_{k}", [P, BANK // 2, PACK], BF16) for k in range(len(quarters))]
            for rounded, raw in zip(pg_bf, quarters):
                round_plain(nc.vector.tensor_copy, rounded[:], raw)
            tag = f"pg_raw{len(page_loads) - 1}" if n else None
            pg_mx.append(quantise(f"pg{n}", [rounded[:] for rounded in pg_bf], tag=tag))
        last_h_tag = "pg_bf1_0"
        h_sb = [sbuf(f"h{r}", [P, Z], F32, tag=last_h_tag if r == PACK - 1 else None) for r in range(PACK)]
        for n, cols in enumerate(halves(Z)):
            for r in range(PACK):
                bank = banks.tile([P, BANK], F32, name="bank")
                product(bank[:], q2_mx, r * P, pg_mx[n], slice(0, BANK))
                empty(PACK * n + r >= SCALAR_PAGE_BANKS, h_sb[r][:, cols], bank[:])

        faded = [sbuf("faded_first", [P, M], F32, tag="pg_bf1_1")]
        fade_on_gpsimd(faded[0], 0)

        def round_messages(k, copy, tag=None):
            rounded = sbuf(f"msg_bf{k}", [P, E // 2, PACK], BF16, tag=tag)
            round_plain(copy, rounded[:], msg_raw[:, :, halves(E)[k]])
            return [rounded[:]]

        groups = halves(I)
        row_pairs = halves(PACK)

        def gather_pages(g):
            tiles = [
                sbuf(f"page_weight{g}_{k}", [P, PACK // 2, GROUP], F32, tag=f"page_weight{k}")
                for k in range(len(row_pairs))
            ]
            for r in range(PACK):
                nc.scalar.activation(
                    out=tiles[r // 2][:, r % 2, :],
                    in_=h_sb[r][:].indirect(page_list[:, entries(groups[g])]),
                    func=SIGMOID,
                )
            return tiles

        def larger(g, k, weight, page_weight):
            rows = row_pairs[k]
            nc.vector.tensor_tensor(
                out=weight[:, rows, :], in0=token_weight[:, rows, groups[g]], in1=page_weight[k][:], op=MAX
            )

        def times_row_factor(g, weight):
            wq_bf = sbuf(f"wq_bf{g}", [P, GROUP, PACK], BF16)
            for cols in halves(GROUP):
                nc.vector.tensor_tensor(
                    out=wq_bf[:, cols, :].rearrange("p (c i) r -> p c r i", i=PACK),
                    in0=weight[:, :, cols].rearrange("p r (c i) -> p c r i", i=PACK),
                    in1=row_factor[:].unsqueeze(1).unsqueeze(3).to_broadcast([P, GROUP // 2 // PACK, PACK, PACK]),
                    op=MULT,
                )
            return [wq_bf[:, cols, :] for cols in halves(GROUP)]

        page_weight = gather_pages(0)
        weight = sbuf("weight0", [P, PACK, GROUP], F32, tag="weight")
        larger(0, 0, weight, page_weight)
        msg_bf = round_messages(0, nc.vector.tensor_copy)
        larger(0, 1, weight, page_weight)
        msg_mx = [quantise("msg0", msg_bf)]
        wq_mx = [quantise("wq0", times_row_factor(0, weight))]

        page_weight = gather_pages(1)
        weight = sbuf("weight1", [P, PACK, GROUP], F32, tag="weight")
        for k in range(len(row_pairs)):
            larger(1, k, weight, page_weight)
        msg_bf = round_messages(1, nc.scalar.copy, tag=last_h_tag)
        wq_bf = times_row_factor(1, weight)
        msg_mx.append(quantise("msg1", msg_bf))
        wq_mx.append(quantise("wq1", wq_bf))

        dl_banks = []
        for group_mx in wq_mx:
            dl_banks.append([])
            for half_mx in msg_mx:
                bank = banks.tile([P, PAIR, GROUP], F32, name="bank")
                for j in range(PAIR):
                    product(bank[:, j, :], half_mx, j * P, group_mx, slice(0, GROUP))
                dl_banks[-1].append(bank)

        late = sbuf("faded_late", [P, E_TILES - 1, M], F32, tag=f"wq_bf{len(groups) - 1}")
        faded.extend(late[:, e - 1, :] for e in range(1, E_TILES))
        fade_on_vector(faded[1], 1)
        for e in range(2, E_TILES):
            fade_on_gpsimd(faded[e], e)

        for g, slots in enumerate(groups):
            last = g == len(groups) - 1
            dl = []
            for k, bank in enumerate(dl_banks[g]):
                staged = sbuf(f"dl{g}_{k}", [P, PAIR, GROUP], F32)
                empty(last, staged[:], bank[:])
                dl.extend(staged[:, j, :] for j in range(PAIR))
            for e in range(E_TILES):
                window = placed[e][:].indirect(column_list[:, entries(slots)])
                if last and e < E_TILES // 2:
                    nc.vector.tensor_copy(out=window, in_=dl[e])
                else:
                    nc.scalar.activation(out=window, in_=dl[e], func=COPY)

        for e in range(E_TILES):
            for cols in halves(M):
                nc.vector.tensor_tensor(out=old_sb[e][:, cols], in0=faded[e][:, cols], in1=placed[e][:, cols], op=ADD)
                nc.sync.dma_start(out=out[e * P : (e + 1) * P, cols], in_=old_sb[e][:, cols])
